import numpy as np
import ml_dtypes


def mxq(x, axis, fmt="e4m3"):
    dtype, down = {"e4m3": (ml_dtypes.float8_e4m3fn, 7), "e5m2": (ml_dtypes.float8_e5m2, 14)}[fmt]
    v = np.moveaxis(np.asarray(x, np.float32).astype(ml_dtypes.bfloat16).astype(np.float64), axis, -1)
    blocks = v.reshape(v.shape[:-1] + (-1, 32))
    amax = np.abs(blocks).max(-1, keepdims=True)
    byte = np.maximum(np.where(amax > 0, np.frexp(amax)[1] - 1 + 127, 0) - down, 1)
    scale = np.exp2(byte - 127.0)
    codes = (blocks / scale).astype(np.float32).astype(dtype).astype(np.float64)
    return np.moveaxis((codes * scale).reshape(v.shape), -1, axis)


WIDE = False


def mx_kscale(k):
    if not WIDE:
        return np.ones(k)
    levels = np.array([10, -10, 5, -5, 0])
    if k % 512:
        return np.exp2(np.random.permutation(np.resize(levels, k // 32))).repeat(32)
    a = np.empty((k // 512, 16))
    for p in range(k // 512):
        a[p, :8] = np.random.permutation(np.resize(levels, 8))
        for g in range(8):
            far = levels[np.abs(levels - a[p, g]) >= 10]
            a[p, g + 8] = far[np.random.randint(len(far))]
    return np.exp2(a.ravel()).repeat(32)


def f64(x):
    return np.asarray(x).astype(np.float64)


def striped(idx):
    return np.tile(idx.reshape(-1, 16).T, (8, 1)).astype(np.uint16)


def unstriped(offs):
    return offs[:16].T.reshape(-1).astype(np.int64)


def striped8(idx):
    return np.concatenate([x.reshape(-1, 16).T for x in idx]).astype(np.uint16)


def runs(offs, k):
    lists = np.stack([offs[16 * r : 16 * r + 16].T.reshape(-1) for r in range(8)]).astype(np.int64)
    return lists[np.arange(k) % 512 // 64]


def pack_weight(w):
    k, n = w.shape
    w = f64(np.asarray(w, np.float32).astype(ml_dtypes.bfloat16)).reshape(k // 32, 32, n)
    amax = np.abs(w).max(1)
    byte = np.clip(np.where(amax > 0, np.frexp(amax)[1] - 1 + 127 - 7, 1), 1, 254)
    scaled = (w * np.exp2(127.0 - byte)[:, None, :]).reshape(k, n).astype(np.float32)
    words = np.ascontiguousarray(scaled.reshape(k // 512, 128, 4, n).transpose(0, 1, 3, 2)).astype(ml_dtypes.float8_e4m3fn).view(np.uint8)
    return words, np.ascontiguousarray(byte.astype(np.uint8).reshape(k // 512, 16, n))


def unpack_weight(words, scales):
    g, p, n, _ = words.shape
    vals = np.ascontiguousarray(words).view(ml_dtypes.float8_e4m3fn).astype(np.float64) * np.repeat(np.exp2(scales.astype(np.float64) - 127.0), 8, axis=1)[..., None]
    return vals.transpose(0, 1, 3, 2).reshape(g * 512, n)


def sigmoid(v):
    return 1.0 / (1.0 + np.exp(-np.maximum(v, -700.0)))


K, T, S, G, H = 512, 2048, 512, 2048, 512


def setup_inputs():
    n = np.random.standard_normal
    s = mx_kscale(K)[:, None]
    packed_xT = pack_weight(n((K, T)) * s)
    packed_dT = pack_weight(n((K, G)) / s)
    return {
        "x_words": packed_xT[0],
        "x_scales": packed_xT[1],
        "d_words": packed_dT[0],
        "d_scales": packed_dT[1],
        "gs": (np.random.uniform(0.5, 1.5, (K, 1)) * s).astype(np.float32),
        "offs": striped(np.random.permutation(T)[:S]),
        "k1": striped8(np.random.randint(0, G, (8, H))),
        "n1": striped8(np.stack([np.random.permutation(S) for _ in range(8)])),
        "n2": striped8(np.stack([np.random.permutation(S) for _ in range(8)])),
        "n3": striped8(np.stack([np.random.permutation(S) for _ in range(8)])),
        "n4": striped8(np.stack([np.random.permutation(S) for _ in range(8)])),
        "n5": striped8(np.stack([np.random.permutation(S) for _ in range(8)])),
        "n6": striped8(np.stack([np.random.permutation(S) for _ in range(8)])),
    }


def reference(x_words, x_scales, d_words, d_scales, gs, offs, k1, n1, n2, n3, n4, n5, n6):
    d_k1 = unpack_weight(d_words, d_scales)[np.arange(K)[:, None], runs(k1, K)]
    xq = unpack_weight(x_words, x_scales)[:, unstriped(offs)]
    h = 0.0625 * (d_k1.T @ xq)
    z = f64(gs) * ((h[np.arange(H)[:, None], runs(n1, H)]) * sigmoid(h) + (h[np.arange(H)[:, None], runs(n2, H)]) * (sigmoid(h[np.arange(H)[:, None], runs(n3, H)])))
    h2 = 0.0625 * ((d_k1.T @ mxq(z, 0, "e4m3")))
    return 0.75 * (h2 * (h2[np.arange(H)[:, None], runs(n4, H)]) + (h2[np.arange(H)[:, None], runs(n5, H)]) * (h2[np.arange(H)[:, None], runs(n6, H)]))

@@ -1,0 +1,158 @@
+from contextlib import ExitStack
+
+import concourse.mybir as mybir
+from concourse.masks import make_identity
+
+F32 = mybir.dt.float32
+BF16 = mybir.dt.bfloat16
+I32 = mybir.dt.int32
+U32 = mybir.dt.uint32
+U16 = mybir.dt.uint16
+U8 = mybir.dt.uint8
+FP8X4 = mybir.dt.float8_e4m3fn_x4
+ACT = mybir.ActivationFunctionType
+ALU = mybir.AluOpType
+
+P = 128
+PACK = 4
+S = 512
+TABLE = 2048
+WINDOW = 1024
+HALF = S // 2
+FLOPS = 2 * 2 * 512 * 512 * 512
+
+
+def tile_picked_ringwsumdot_none_p_kernel(tc, x_words, x_scales, d_words, d_scales, gs, offs, k1, n1, n2, n3, n4, n5, n6, out):
+    nc = tc.nc
+    with ExitStack() as ctx:
+        held = ctx.enter_context(tc.tile_pool(name="held", bufs=1))
+        psum = ctx.enter_context(tc.psum_pool(name="psum", bufs=1))
+
+        def load_list(name, src):
+            tile = held.tile([P, S // 16], U16, name=name)
+            nc.sync.dma_start(tile[:], src)
+            return tile
+
+        def load_words(name, src):
+            tile = held.tile([P, TABLE], U32, name=name)
+            nc.sync.dma_start(tile[:].bitcast(I32), src[0].rearrange("p n r -> p (n r)").bitcast(I32))
+            return tile
+
+        def load_bytes(name, src, eng):
+            tile = held.tile([P, TABLE], U8, name=name)
+            eng.memset(tile[:].bitcast(I32), 0)
+            nc.sync.dma_start(tile[0:P:8, :].bitcast(I32), src[0].bitcast(I32))
+            return tile
+
+        k1_list = load_list("k1_list", k1)
+        offs_list = load_list("offs_list", offs)
+        d_byte_table = load_bytes("d_byte_table", d_scales, nc.gpsimd)
+        x_byte_table = load_bytes("x_byte_table", x_scales, nc.vector)
+        n3_list = load_list("n3_list", n3)
+        n1_list = load_list("n1_list", n1)
+        n2_list = load_list("n2_list", n2)
+        d_word_table = load_words("d_word_table", d_words)
+        x_word_table = load_words("x_word_table", x_words)
+        gs_cols = held.tile([P, PACK], F32, name="gs_cols")
+        nc.gpsimd.dma_start(gs_cols[:], gs.rearrange("(p t) o -> p (t o)", t=PACK))
+        n5_list = load_list("n5_list", n5)
+        n4_list = load_list("n4_list", n4)
+        n6_list = load_list("n6_list", n6)
+
+        planes = held.tile([P, 2 * S], U8, name="planes", align_bytes=64)
+        nc.vector.memset(planes[:].bitcast(I32), 0)
+        warm = held.tile([P, 2], F32, name="warm")
+        nc.vector.memset(warm[:, 0:1], 0.0)
+        nc.scalar.activation(warm[:, 1:2], warm[:, 0:1], ACT.Sigmoid)
+
+        raw_win = [held.tile([P, WINDOW], F32, name=f"raw_win{t}") for t in range(PACK)]
+        gain_win = [held.tile([P, WINDOW], F32, name=f"gain_win{t}") for t in range(PACK)]
+        for t in range(PACK):
+            nc.gpsimd.memset(gain_win[t][:, S:], 0.0)
+        identity = held.tile([P, P], F32, name="identity")
+        make_identity(nc, identity[:])
+
+        d_bytes = held.tile([P, S], U8, name="d_bytes")
+        x_bytes = held.tile([P, S], U8, name="x_bytes")
+        staged = held.tile([P, 2 * S], U8, name="staged")
+        nc.vector.tensor_copy(d_bytes[:], d_byte_table[:].indirect(k1_list[:]))
+        nc.vector.tensor_copy(staged[:, :S].rearrange("p (t m) -> p m t", t=PACK), d_bytes[:].rearrange("p (m t) -> p m t", t=PACK))
+        nc.vector.tensor_copy(x_bytes[:], x_byte_table[:].indirect(offs_list[:]))
+        nc.vector.tensor_copy(staged[:, S:], x_bytes[:])
+        for r in range(4):
+            nc.scalar.dma_start(planes[r:P:32, :].bitcast(I32), staged[8 * r : P : 32, :].bitcast(I32))
+
+        d_picked = held.tile([P, S], U32, name="d_picked")
+        d_codes = held.tile([P, S], U32, name="d_codes", align_bytes=64)
+        x_codes = held.tile([P, S], U32, name="x_codes", align_bytes=64)
+        nc.vector.tensor_copy(d_picked[:], d_word_table[:].indirect(k1_list[:]))
+        nc.vector.tensor_copy(d_codes[:].rearrange("p (t m) -> p m t", t=PACK), d_picked[:].rearrange("p (m t) -> p m t", t=PACK))
+        halves = [slice(0, HALF), slice(HALF, S)]
+        list_halves = [slice(0, HALF // 16), slice(HALF // 16, S // 16)]
+        for u in range(2):
+            nc.vector.tensor_copy(x_codes[:, halves[u]], x_word_table[:].indirect(offs_list[:, list_halves[u]]))
+
+        def product(bank, t, codes, scales):
+            cols = slice(t * P, (t + 1) * P)
+            nc.tensor.matmul_mx(bank, lhsT=d_codes[:, cols].bitcast(FP8X4), lhsT_scale=planes[:, cols],
+                                rhs=codes.bitcast(FP8X4), rhs_scale=scales, start=True, stop=True)
+
+        x_planes = planes[:, S:]
+        a4 = held.tile([P, PACK, S], F32, name="a4")
+        b4 = held.tile([P, PACK, S], F32, name="b4")
+        for t in range(PACK):
+            bank = psum.tile([P, S], F32, name=f"h{t}")
+            raw = raw_win[t][:, :S]
+            sig = raw_win[t][:, S:]
+            gain = gain_win[t][:, :S]
+            sig3 = held.tile([P, S], F32, name=f"sig3_{t}")
+            for cols in (halves if t == 0 else [slice(0, S)]):
+                product(bank[:, cols], t, x_codes[:, cols], x_planes[:, cols])
+                nc.scalar.copy(raw[:, cols], bank[:, cols])
+                nc.scalar.activation(sig[:, cols], bank[:, cols], ACT.Sigmoid, scale=0.0625)
+                nc.vector.tensor_scalar(gain[:, cols], raw[:, cols], gs_cols[:, t : t + 1], 0.0625, ALU.mult, ALU.mult)
+            nc.scalar.activation(sig3[:], raw_win[t][:].indirect(n3_list[:]), ACT.Sigmoid, scale=0.0625)
+            nc.vector.tensor_tensor(a4[:, t, :], gain_win[t][:].indirect(n1_list[:]), sig, ALU.mult)
+            nc.vector.tensor_tensor(b4[:, t, :], gain_win[t][:].indirect(n2_list[:]), sig3[:], ALU.mult)
+
+        z_codes = held.tile([P, S], U32, name="z_codes", align_bytes=64)
+        z_scales = held.tile([P, S], U8, name="z_scales", align_bytes=64)
+        banks = [psum.tile([P, S], F32, name=f"g{t}") for t in range(PACK)]
+        for u, cols in enumerate(halves):
+            zb = held.tile([P, HALF, PACK], BF16, name=f"zb{u}", align_bytes=64)
+            nc.vector.tensor_tensor(zb[:].rearrange("p (c i) t -> p c t i", i=4),
+                                    a4[:, :, cols].rearrange("p t (c i) -> p c t i", i=4),
+                                    b4[:, :, cols].rearrange("p t (c i) -> p c t i", i=4), ALU.add)
+            nc.vector.quantize_mx(z_codes[:, cols].bitcast(FP8X4), z_scales[:, cols], zb[:].rearrange("p j t -> p (j t)"))
+            for t in range(PACK):
+                product(banks[t][:, cols], t, z_codes[:, cols], z_scales[:, cols])
+                nc.scalar.activation(raw_win[t][:, cols], banks[t][:, cols], ACT.Copy, scale=0.0625 * 0.75)
+                nc.scalar.activation(gain_win[t][:, cols], banks[t][:, cols], ACT.Copy, scale=0.0625)
+
+        out_rows = out.rearrange("(p t) j -> p t j", t=PACK)
+        for t in range(PACK):
+            scaled, win = raw_win[t], gain_win[t]
+            c = held.tile([P, S], F32, name=f"c{t}")
+            a = held.tile([P, S], F32, name=f"a2_{t}")
+            b = held.tile([P, S], F32, name=f"b2_{t}")
+            o = held.tile([P, S], F32, name=f"o{t}")
+            nc.vector.tensor_copy(c[:], scaled[:].indirect(n5_list[:]))
+            nc.vector.tensor_tensor(a[:], win[:].indirect(n4_list[:]), scaled[:, :S], ALU.mult)
+            if t < PACK - 1:
+                nc.vector.tensor_tensor(b[:], win[:].indirect(n6_list[:]), c[:], ALU.mult)
+                turned = psum.tile([P, S], F32, name=f"h{t % 2}")
+                for j in range(0, S, P):
+                    for k, term in enumerate((a, b)):
+                        nc.tensor.matmul(turned[:, j : j + P], term[:, j : j + P], identity[:], start=(k == 0), stop=(k == 1), is_transpose=True)
+                summed = held.tile([P, S], F32, name=f"summed{t}")
+                nc.scalar.copy(summed[:], turned[:])
+                back = psum.tile([P, S], F32, name=f"h{2 + t % 2}")
+                for j in range(0, S, P):
+                    nc.tensor.transpose(back[:, j : j + P], summed[:, j : j + P], identity[:])
+                nc.scalar.copy(o[:], back[:])
+                nc.sync.dma_start(out_rows[:, t, :], o[:])
+            else:
+                for u, cols in enumerate(halves):
+                    nc.vector.tensor_tensor(b[:, cols], win[:].indirect(n6_list[:, list_halves[u]]), c[:, cols], ALU.mult)
+                    nc.vector.tensor_tensor(o[:, cols], a[:, cols], b[:, cols], ALU.add)
+                    nc.sync.dma_start(out_rows[:, t, cols], o[:, cols])

@@ -38,29 +38,29 @@ def tile_picked_ringwsumdot_none_p_kernel(tc, x_words, x_scales, d_words, d_scal
             nc.sync.dma_start(tile[:].bitcast(I32), src[0].rearrange("p n r -> p (n r)").bitcast(I32))
             return tile
 
-        def load_bytes(name, src, eng):
-            tile = held.tile([P, TABLE], U8, name=name)
-            eng.memset(tile[:].bitcast(I32), 0)
-            nc.sync.dma_start(tile[0:P:8, :].bitcast(I32), src[0].bitcast(I32))
-            return tile
-
+        d_byte_table = held.tile([P, TABLE], U8, name="d_byte_table")
+        x_byte_table = held.tile([P, TABLE], U8, name="x_byte_table")
+        nc.gpsimd.memset(d_byte_table[:].bitcast(I32), 0)
+        nc.vector.memset(x_byte_table[:].bitcast(I32), 0)
+        nc.sync.dma_start(d_byte_table[0:P:8, :].bitcast(I32), d_scales[0].bitcast(I32))
         k1_list = load_list("k1_list", k1)
         offs_list = load_list("offs_list", offs)
-        d_byte_table = load_bytes("d_byte_table", d_scales, nc.gpsimd)
-        x_byte_table = load_bytes("x_byte_table", x_scales, nc.vector)
+        for q in range(4):
+            nc.sync.dma_start(x_byte_table[32 * q : 32 * q + 4, :].bitcast(I32), x_scales[0, 4 * q : 4 * q + 4, :].bitcast(I32))
+        d_word_table = load_words("d_word_table", d_words)
+        x_word_table = load_words("x_word_table", x_words)
         n3_list = load_list("n3_list", n3)
         n1_list = load_list("n1_list", n1)
         n2_list = load_list("n2_list", n2)
-        d_word_table = load_words("d_word_table", d_words)
-        x_word_table = load_words("x_word_table", x_words)
         gs_cols = held.tile([P, PACK], F32, name="gs_cols")
         nc.gpsimd.dma_start(gs_cols[:], gs.rearrange("(p t) o -> p (t o)", t=PACK))
+        gains = held.tile([P, PACK], F32, name="gains")
+        nc.gpsimd.tensor_scalar(gains[:], gs_cols[:], 0.0625, 0.0, ALU.mult, ALU.add)
         n5_list = load_list("n5_list", n5)
         n4_list = load_list("n4_list", n4)
         n6_list = load_list("n6_list", n6)
 
-        planes = held.tile([P, 2 * S], U8, name="planes", align_bytes=64)
-        nc.vector.memset(planes[:].bitcast(I32), 0)
+        planes = held.tile([P, S], U8, name="planes", align_bytes=64)
         warm = held.tile([P, 2], F32, name="warm")
         nc.vector.memset(warm[:, 0:1], 0.0)
         nc.scalar.activation(warm[:, 1:2], warm[:, 0:1], ACT.Sigmoid)
@@ -73,14 +73,12 @@ def tile_picked_ringwsumdot_none_p_kernel(tc, x_words, x_scales, d_words, d_scal
         make_identity(nc, identity[:])
 
         d_bytes = held.tile([P, S], U8, name="d_bytes")
-        x_bytes = held.tile([P, S], U8, name="x_bytes")
-        staged = held.tile([P, 2 * S], U8, name="staged")
+        x_planes = held.tile([P, S], U8, name="x_planes", align_bytes=64)
         nc.vector.tensor_copy(d_bytes[:], d_byte_table[:].indirect(k1_list[:]))
-        nc.vector.tensor_copy(staged[:, :S].rearrange("p (t m) -> p m t", t=PACK), d_bytes[:].rearrange("p (m t) -> p m t", t=PACK))
-        nc.vector.tensor_copy(x_bytes[:], x_byte_table[:].indirect(offs_list[:]))
-        nc.vector.tensor_copy(staged[:, S:], x_bytes[:])
-        for r in range(4):
-            nc.scalar.dma_start(planes[r:P:32, :].bitcast(I32), staged[8 * r : P : 32, :].bitcast(I32))
+        nc.vector.tensor_copy(planes[:].rearrange("p (t m) -> p m t", t=PACK), d_bytes[:].rearrange("p (m t) -> p m t", t=PACK))
+        for r in range(1, 4):
+            nc.scalar.dma_start(planes[r:P:32, :].bitcast(I32), planes[8 * r : P : 32, :].bitcast(I32))
+        nc.vector.tensor_copy(x_planes[:], x_byte_table[:].indirect(offs_list[:]))
 
         d_picked = held.tile([P, S], U32, name="d_picked")
         d_codes = held.tile([P, S], U32, name="d_codes", align_bytes=64)
@@ -97,37 +95,77 @@ def tile_picked_ringwsumdot_none_p_kernel(tc, x_words, x_scales, d_words, d_scal
             nc.tensor.matmul_mx(bank, lhsT=d_codes[:, cols].bitcast(FP8X4), lhsT_scale=planes[:, cols],
                                 rhs=codes.bitcast(FP8X4), rhs_scale=scales, start=True, stop=True)
 
-        x_planes = planes[:, S:]
         a4 = held.tile([P, PACK, S], F32, name="a4")
         b4 = held.tile([P, PACK, S], F32, name="b4")
-        for t in range(PACK):
-            bank = psum.tile([P, S], F32, name=f"h{t}")
+
+        def new_bank(index, shape=(P, S)):
+            return psum.tile(list(shape), F32, name=f"bank{index}")
+
+        whole = slice(0, S)
+
+        def own_term(t):
             raw = raw_win[t][:, :S]
             sig = raw_win[t][:, S:]
             gain = gain_win[t][:, :S]
-            sig3 = held.tile([P, S], F32, name=f"sig3_{t}")
-            for cols in (halves if t == 0 else [slice(0, S)]):
+            pieces = [(0, halves[0]), (1, halves[1])] if t == 0 else [(t + 1, whole)]
+            for index, cols in pieces:
+                bank = new_bank(index)
                 product(bank[:, cols], t, x_codes[:, cols], x_planes[:, cols])
                 nc.scalar.copy(raw[:, cols], bank[:, cols])
                 nc.scalar.activation(sig[:, cols], bank[:, cols], ACT.Sigmoid, scale=0.0625)
-                nc.vector.tensor_scalar(gain[:, cols], raw[:, cols], gs_cols[:, t : t + 1], 0.0625, ALU.mult, ALU.mult)
-            nc.scalar.activation(sig3[:], raw_win[t][:].indirect(n3_list[:]), ACT.Sigmoid, scale=0.0625)
+                if t < PACK - 1:
+                    nc.vector.tensor_scalar(gain[:, cols], raw[:, cols], gains[:, t : t + 1], None, ALU.mult)
+                else:
+                    nc.scalar.activation(gain[:, cols], bank[:, cols], ACT.Copy, scale=gains[:, t : t + 1])
             nc.vector.tensor_tensor(a4[:, t, :], gain_win[t][:].indirect(n1_list[:]), sig, ALU.mult)
-            nc.vector.tensor_tensor(b4[:, t, :], gain_win[t][:].indirect(n2_list[:]), sig3[:], ALU.mult)
+
+        blocks = [slice(0, P), slice(P, 2 * P)]
+        turned_z = [new_bank(5 + jb, (P, PACK, P)) for jb in range(2)]
+
+        def far_term(t):
+            sig3 = held.tile([P, S], F32, name=f"sig3_{t}")
+            nc.scalar.activation(sig3[:], raw_win[t][:].indirect(n3_list[:]), ACT.Sigmoid, scale=0.0625)
+            pieces = list(zip(halves, list_halves)) if t == PACK - 1 else [(whole, slice(0, S // 16))]
+            for cols, entries in pieces:
+                nc.vector.tensor_tensor(b4[:, t, cols], gain_win[t][:].indirect(n2_list[:, entries]), sig3[:, cols], ALU.mult)
+            for jb in range(2):
+                for k, term in enumerate((a4, b4)):
+                    nc.tensor.matmul(turned_z[jb][:, t, :], term[:, t, blocks[jb]], identity[:], start=(k == 0), stop=(k == 1), is_transpose=True)
+
+        for t in range(PACK + 1):
+            if t < PACK:
+                own_term(t)
+            if t > 0:
+                far_term(t - 1)
 
         z_codes = held.tile([P, S], U32, name="z_codes", align_bytes=64)
         z_scales = held.tile([P, S], U8, name="z_scales", align_bytes=64)
-        banks = [psum.tile([P, S], F32, name=f"g{t}") for t in range(PACK)]
-        for u, cols in enumerate(halves):
-            zb = held.tile([P, HALF, PACK], BF16, name=f"zb{u}", align_bytes=64)
-            nc.vector.tensor_tensor(zb[:].rearrange("p (c i) t -> p c t i", i=4),
-                                    a4[:, :, cols].rearrange("p t (c i) -> p c t i", i=4),
-                                    b4[:, :, cols].rearrange("p t (c i) -> p c t i", i=4), ALU.add)
-            nc.vector.quantize_mx(z_codes[:, cols].bitcast(FP8X4), z_scales[:, cols], zb[:].rearrange("p j t -> p (j t)"))
-            for t in range(PACK):
-                product(banks[t][:, cols], t, z_codes[:, cols], z_scales[:, cols])
-                nc.scalar.activation(raw_win[t][:, cols], banks[t][:, cols], ACT.Copy, scale=0.0625 * 0.75)
-                nc.scalar.activation(gain_win[t][:, cols], banks[t][:, cols], ACT.Copy, scale=0.0625)
+        zb = [held.tile([P, HALF, PACK], BF16, name=f"zb{u}", align_bytes=64) for u in range(2)]
+        pairs = [held.tile([P, 2, P, 2], BF16, name=f"pairs{jb}") for jb in range(2)]
+        for jb in range(2):
+            nc.scalar.copy(pairs[jb][:], turned_z[jb][:].rearrange("j (u e) p -> j u p e", e=2))
+        zb_words = zb[0][:].rearrange("p j t -> p (j t)").bitcast(F32).rearrange("p (j u) -> p j u", u=2)
+        for jb in range(2):
+            words = pairs[jb][:].rearrange("j u p e -> j (u p e)").bitcast(F32)
+            back = new_bank((7, 0)[jb], (P, 2, P))
+            for u in range(2):
+                nc.tensor.transpose(back[:, u, :], words[:, u * P : (u + 1) * P], identity[:])
+            nc.scalar.copy(zb_words[:, blocks[jb], :], back[:].rearrange("p u j -> p j u"))
+        nc.vector.tensor_tensor(zb[1][:].rearrange("p (c i) t -> p c t i", i=4),
+                                a4[:, :, halves[1]].rearrange("p t (c i) -> p c t i", i=4),
+                                b4[:, :, halves[1]].rearrange("p t (c i) -> p c t i", i=4), ALU.add)
+
+        def second_product(index, t, cols):
+            bank = new_bank(index)
+            product(bank[:, cols], t, z_codes[:, cols], z_scales[:, cols])
+            nc.scalar.activation(raw_win[t][:, cols], bank[:, cols], ACT.Copy, scale=0.0625 * 0.75)
+            nc.scalar.activation(gain_win[t][:, cols], bank[:, cols], ACT.Copy, scale=0.0625)
+
+        for u in (1, 0):
+            nc.vector.quantize_mx(z_codes[:, halves[u]].bitcast(FP8X4), z_scales[:, halves[u]], zb[u][:].rearrange("p j t -> p (j t)"))
+            second_product(u, 0, halves[u])
+        for t in range(1, PACK):
+            second_product(t + 1, t, whole)
 
         out_rows = out.rearrange("(p t) j -> p t j", t=PACK)
         for t in range(PACK):
@@ -140,13 +178,13 @@ def tile_picked_ringwsumdot_none_p_kernel(tc, x_words, x_scales, d_words, d_scal
             nc.vector.tensor_tensor(a[:], win[:].indirect(n4_list[:]), scaled[:, :S], ALU.mult)
             if t < PACK - 1:
                 nc.vector.tensor_tensor(b[:], win[:].indirect(n6_list[:]), c[:], ALU.mult)
-                turned = psum.tile([P, S], F32, name=f"h{t % 2}")
+                turned = new_bank(5 + t % 2)
                 for j in range(0, S, P):
                     for k, term in enumerate((a, b)):
                         nc.tensor.matmul(turned[:, j : j + P], term[:, j : j + P], identity[:], start=(k == 0), stop=(k == 1), is_transpose=True)
                 summed = held.tile([P, S], F32, name=f"summed{t}")
                 nc.scalar.copy(summed[:], turned[:])
-                back = psum.tile([P, S], F32, name=f"h{2 + t % 2}")
+                back = new_bank((7, 1)[t % 2])
                 for j in range(0, S, P):
                     nc.tensor.transpose(back[:, j : j + P], summed[:, j : j + P], identity[:])
                 nc.scalar.copy(o[:], back[:])

@@ -15,21 +15,40 @@ ALU = mybir.AluOpType
 
 P = 128
 PACK = 4
+LAST = PACK - 1
 S = 512
-TABLE = 2048
-WINDOW = 1024
 HALF = S // 2
+GROUP = 16
+QUADRANT = 32
+BLOCK_PARTITIONS = 8
+TABLE = 2048
+WINDOW = 2 * S
+SIXTEENTH = 0.0625
+OUT_FACTOR = 0.75
+
+FIRST_TILE_BANKS = (0, 1)
+TURN_BANKS = (5, 6)
+BACK_BANKS = (7, 0)
+SECOND_FIRST_TILE_BANKS = (1, 5, 6)
+
 FLOPS = 2 * 2 * 512 * 512 * 512
 
 
 def tile_picked_ringwsumdot_none_p_kernel(tc, x_words, x_scales, d_words, d_scales, gs, offs, k1, n1, n2, n3, n4, n5, n6, out):
     nc = tc.nc
+    whole = slice(0, S)
+    halves = [slice(0, HALF), slice(HALF, S)]
+    squares = [slice(0, P), slice(P, 2 * P)]
+
+    def entries(cols):
+        return slice(cols.start // GROUP, cols.stop // GROUP)
+
     with ExitStack() as ctx:
         held = ctx.enter_context(tc.tile_pool(name="held", bufs=1))
         psum = ctx.enter_context(tc.psum_pool(name="psum", bufs=1))
 
         def load_list(name, src):
-            tile = held.tile([P, S // 16], U16, name=name)
+            tile = held.tile([P, S // GROUP], U16, name=name)
             nc.sync.dma_start(tile[:], src)
             return tile
 
@@ -38,15 +57,18 @@ def tile_picked_ringwsumdot_none_p_kernel(tc, x_words, x_scales, d_words, d_scal
             nc.sync.dma_start(tile[:].bitcast(I32), src[0].rearrange("p n r -> p (n r)").bitcast(I32))
             return tile
 
+        def new_bank(index, shape=(P, S)):
+            return psum.tile(list(shape), F32, name=f"bank{index}")
+
         d_byte_table = held.tile([P, TABLE], U8, name="d_byte_table")
         x_byte_table = held.tile([P, TABLE], U8, name="x_byte_table")
         nc.gpsimd.memset(d_byte_table[:].bitcast(I32), 0)
         nc.vector.memset(x_byte_table[:].bitcast(I32), 0)
-        nc.sync.dma_start(d_byte_table[0:P:8, :].bitcast(I32), d_scales[0].bitcast(I32))
+        nc.sync.dma_start(d_byte_table[0:P:BLOCK_PARTITIONS, :].bitcast(I32), d_scales[0].bitcast(I32))
         k1_list = load_list("k1_list", k1)
         offs_list = load_list("offs_list", offs)
-        for q in range(4):
-            nc.sync.dma_start(x_byte_table[32 * q : 32 * q + 4, :].bitcast(I32), x_scales[0, 4 * q : 4 * q + 4, :].bitcast(I32))
+        for q in range(P // QUADRANT):
+            nc.sync.dma_start(x_byte_table[QUADRANT * q : QUADRANT * q + 4, :].bitcast(I32), x_scales[0, 4 * q : 4 * q + 4, :].bitcast(I32))
         d_word_table = load_words("d_word_table", d_words)
         x_word_table = load_words("x_word_table", x_words)
         n3_list = load_list("n3_list", n3)
@@ -55,142 +77,145 @@ def tile_picked_ringwsumdot_none_p_kernel(tc, x_words, x_scales, d_words, d_scal
         gs_cols = held.tile([P, PACK], F32, name="gs_cols")
         nc.gpsimd.dma_start(gs_cols[:], gs.rearrange("(p t) o -> p (t o)", t=PACK))
         gains = held.tile([P, PACK], F32, name="gains")
-        nc.gpsimd.tensor_scalar(gains[:], gs_cols[:], 0.0625, 0.0, ALU.mult, ALU.add)
+        nc.gpsimd.tensor_scalar(gains[:], gs_cols[:], SIXTEENTH, 0.0, ALU.mult, ALU.add)
         n5_list = load_list("n5_list", n5)
         n4_list = load_list("n4_list", n4)
         n6_list = load_list("n6_list", n6)
 
-        planes = held.tile([P, S], U8, name="planes", align_bytes=64)
-        warm = held.tile([P, 2], F32, name="warm")
-        nc.vector.memset(warm[:, 0:1], 0.0)
-        nc.scalar.activation(warm[:, 1:2], warm[:, 0:1], ACT.Sigmoid)
+        d_scale_rows = held.tile([P, S], U8, name="d_scale_rows", align_bytes=64)
 
-        raw_win = [held.tile([P, WINDOW], F32, name=f"raw_win{t}") for t in range(PACK)]
-        gain_win = [held.tile([P, WINDOW], F32, name=f"gain_win{t}") for t in range(PACK)]
+        window_a = [held.tile([P, WINDOW], F32, name=f"window_a{t}") for t in range(PACK)]
+        window_b = [held.tile([P, WINDOW], F32, name=f"window_b{t}") for t in range(PACK)]
         for t in range(PACK):
-            nc.gpsimd.memset(gain_win[t][:, S:], 0.0)
+            nc.gpsimd.memset(window_b[t][:, S:], 0.0)
         identity = held.tile([P, P], F32, name="identity")
         make_identity(nc, identity[:])
 
         d_bytes = held.tile([P, S], U8, name="d_bytes")
-        x_planes = held.tile([P, S], U8, name="x_planes", align_bytes=64)
+        x_scale_rows = held.tile([P, S], U8, name="x_scale_rows", align_bytes=64)
         nc.vector.tensor_copy(d_bytes[:], d_byte_table[:].indirect(k1_list[:]))
-        nc.vector.tensor_copy(planes[:].rearrange("p (t m) -> p m t", t=PACK), d_bytes[:].rearrange("p (m t) -> p m t", t=PACK))
+        nc.vector.tensor_copy(d_scale_rows[:].rearrange("p (t m) -> p m t", t=PACK), d_bytes[:].rearrange("p (m t) -> p m t", t=PACK))
         for r in range(1, 4):
-            nc.scalar.dma_start(planes[r:P:32, :].bitcast(I32), planes[8 * r : P : 32, :].bitcast(I32))
-        nc.vector.tensor_copy(x_planes[:], x_byte_table[:].indirect(offs_list[:]))
+            nc.scalar.dma_start(d_scale_rows[r:P:QUADRANT, :].bitcast(I32), d_scale_rows[BLOCK_PARTITIONS * r : P : QUADRANT, :].bitcast(I32))
+        nc.vector.tensor_copy(x_scale_rows[:], x_byte_table[:].indirect(offs_list[:]))
 
         d_picked = held.tile([P, S], U32, name="d_picked")
         d_codes = held.tile([P, S], U32, name="d_codes", align_bytes=64)
         x_codes = held.tile([P, S], U32, name="x_codes", align_bytes=64)
         nc.vector.tensor_copy(d_picked[:], d_word_table[:].indirect(k1_list[:]))
-        nc.vector.tensor_copy(d_codes[:].rearrange("p (t m) -> p m t", t=PACK), d_picked[:].rearrange("p (m t) -> p m t", t=PACK))
-        halves = [slice(0, HALF), slice(HALF, S)]
-        list_halves = [slice(0, HALF // 16), slice(HALF // 16, S // 16)]
-        for u in range(2):
-            nc.vector.tensor_copy(x_codes[:, halves[u]], x_word_table[:].indirect(offs_list[:, list_halves[u]]))
+        dealt = d_codes[:].rearrange("p (t m) -> p m t", t=PACK)
+        picked = d_picked[:].rearrange("p (m t) -> p m t", t=PACK)
+        nc.vector.tensor_copy(dealt[:, :, 0], picked[:, :, 0])
+        for cols in halves:
+            nc.vector.tensor_copy(x_codes[:, cols], x_word_table[:].indirect(offs_list[:, entries(cols)]))
+        nc.vector.tensor_copy(dealt[:, :, 1:], picked[:, :, 1:])
 
         def product(bank, t, codes, scales):
-            cols = slice(t * P, (t + 1) * P)
-            nc.tensor.matmul_mx(bank, lhsT=d_codes[:, cols].bitcast(FP8X4), lhsT_scale=planes[:, cols],
+            rows = slice(t * P, (t + 1) * P)
+            nc.tensor.matmul_mx(bank, lhsT=d_codes[:, rows].bitcast(FP8X4), lhsT_scale=d_scale_rows[:, rows],
                                 rhs=codes.bitcast(FP8X4), rhs_scale=scales, start=True, stop=True)
 
-        a4 = held.tile([P, PACK, S], F32, name="a4")
-        b4 = held.tile([P, PACK, S], F32, name="b4")
+        term1 = held.tile([P, PACK, S], F32, name="term1")
+        term2 = held.tile([P, PACK, S], F32, name="term2")
 
-        def new_bank(index, shape=(P, S)):
-            return psum.tile(list(shape), F32, name=f"bank{index}")
-
-        whole = slice(0, S)
-
-        def own_term(t):
-            raw = raw_win[t][:, :S]
-            sig = raw_win[t][:, S:]
-            gain = gain_win[t][:, :S]
-            pieces = [(0, halves[0]), (1, halves[1])] if t == 0 else [(t + 1, whole)]
+        def make_term1(t):
+            sums = window_a[t][:, :S]
+            sig = window_a[t][:, S:]
+            weighted = window_b[t][:, :S]
+            pieces = list(zip(FIRST_TILE_BANKS, halves)) if t == 0 else [(t + 1, whole)]
             for index, cols in pieces:
                 bank = new_bank(index)
-                product(bank[:, cols], t, x_codes[:, cols], x_planes[:, cols])
-                nc.scalar.copy(raw[:, cols], bank[:, cols])
-                nc.scalar.activation(sig[:, cols], bank[:, cols], ACT.Sigmoid, scale=0.0625)
-                if t < PACK - 1:
-                    nc.vector.tensor_scalar(gain[:, cols], raw[:, cols], gains[:, t : t + 1], None, ALU.mult)
+                product(bank[:, cols], t, x_codes[:, cols], x_scale_rows[:, cols])
+                sigmoid_first = t == 0 and cols == halves[0]
+                if sigmoid_first:
+                    nc.scalar.activation(sig[:, cols], bank[:, cols], ACT.Sigmoid, scale=SIXTEENTH)
+                nc.scalar.copy(sums[:, cols], bank[:, cols])
+                if not sigmoid_first:
+                    nc.scalar.activation(sig[:, cols], bank[:, cols], ACT.Sigmoid, scale=SIXTEENTH)
+                if t < LAST:
+                    nc.vector.tensor_scalar(weighted[:, cols], sums[:, cols], gains[:, t : t + 1], None, ALU.mult)
                 else:
-                    nc.scalar.activation(gain[:, cols], bank[:, cols], ACT.Copy, scale=gains[:, t : t + 1])
-            nc.vector.tensor_tensor(a4[:, t, :], gain_win[t][:].indirect(n1_list[:]), sig, ALU.mult)
+                    nc.scalar.activation(weighted[:, cols], bank[:, cols], ACT.Copy, scale=gains[:, t : t + 1])
+            nc.vector.tensor_tensor(term1[:, t, :], window_b[t][:].indirect(n1_list[:]), sig, ALU.mult)
 
-        blocks = [slice(0, P), slice(P, 2 * P)]
-        turned_z = [new_bank(5 + jb, (P, PACK, P)) for jb in range(2)]
+        turned_z = [new_bank(index, (P, PACK, P)) for index in TURN_BANKS]
 
-        def far_term(t):
-            sig3 = held.tile([P, S], F32, name=f"sig3_{t}")
-            nc.scalar.activation(sig3[:], raw_win[t][:].indirect(n3_list[:]), ACT.Sigmoid, scale=0.0625)
-            pieces = list(zip(halves, list_halves)) if t == PACK - 1 else [(whole, slice(0, S // 16))]
-            for cols, entries in pieces:
-                nc.vector.tensor_tensor(b4[:, t, cols], gain_win[t][:].indirect(n2_list[:, entries]), sig3[:, cols], ALU.mult)
-            for jb in range(2):
-                for k, term in enumerate((a4, b4)):
-                    nc.tensor.matmul(turned_z[jb][:, t, :], term[:, t, blocks[jb]], identity[:], start=(k == 0), stop=(k == 1), is_transpose=True)
+        def make_term2(t):
+            sig_n3 = held.tile([P, S], F32, name=f"sig_n3_{t}")
+            nc.scalar.activation(sig_n3[:], window_a[t][:].indirect(n3_list[:]), ACT.Sigmoid, scale=SIXTEENTH)
+            for cols in halves if t == LAST else [whole]:
+                nc.vector.tensor_tensor(term2[:, t, cols], window_b[t][:].indirect(n2_list[:, entries(cols)]), sig_n3[:, cols], ALU.mult)
+            for turned, square in zip(turned_z, squares):
+                for k, term in enumerate((term1, term2)):
+                    nc.tensor.matmul(turned[:, t, :], term[:, t, square], identity[:], start=(k == 0), stop=(k == 1), is_transpose=True)
 
         for t in range(PACK + 1):
             if t < PACK:
-                own_term(t)
+                make_term1(t)
             if t > 0:
-                far_term(t - 1)
+                make_term2(t - 1)
 
         z_codes = held.tile([P, S], U32, name="z_codes", align_bytes=64)
-        z_scales = held.tile([P, S], U8, name="z_scales", align_bytes=64)
-        zb = [held.tile([P, HALF, PACK], BF16, name=f"zb{u}", align_bytes=64) for u in range(2)]
-        pairs = [held.tile([P, 2, P, 2], BF16, name=f"pairs{jb}") for jb in range(2)]
-        for jb in range(2):
-            nc.scalar.copy(pairs[jb][:], turned_z[jb][:].rearrange("j (u e) p -> j u p e", e=2))
-        zb_words = zb[0][:].rearrange("p j t -> p (j t)").bitcast(F32).rearrange("p (j u) -> p j u", u=2)
-        for jb in range(2):
-            words = pairs[jb][:].rearrange("j u p e -> j (u p e)").bitcast(F32)
-            back = new_bank((7, 0)[jb], (P, 2, P))
+        z_scale_rows = held.tile([P, S], U8, name="z_scale_rows", align_bytes=64)
+        z_half = [held.tile([P, HALF, PACK], BF16, name=f"z_half{u}", align_bytes=64) for u in range(2)]
+        pairs = [held.tile([P, 2, P, 2], BF16, name=f"pairs{i}") for i in range(2)]
+        for paired, turned in zip(pairs, turned_z):
+            nc.scalar.copy(paired[:], turned[:].rearrange("j (u e) p -> j u p e", e=2))
+        z_pairs = z_half[0][:].rearrange("p j t -> p (j t)").bitcast(F32).rearrange("p (j u) -> p j u", u=2)
+        for paired, index, square in zip(pairs, BACK_BANKS, squares):
+            moved = paired[:].rearrange("j u p e -> j (u p e)").bitcast(F32)
+            back = new_bank(index, (P, 2, P))
             for u in range(2):
-                nc.tensor.transpose(back[:, u, :], words[:, u * P : (u + 1) * P], identity[:])
-            nc.scalar.copy(zb_words[:, blocks[jb], :], back[:].rearrange("p u j -> p j u"))
-        nc.vector.tensor_tensor(zb[1][:].rearrange("p (c i) t -> p c t i", i=4),
-                                a4[:, :, halves[1]].rearrange("p t (c i) -> p c t i", i=4),
-                                b4[:, :, halves[1]].rearrange("p t (c i) -> p c t i", i=4), ALU.add)
+                nc.tensor.transpose(back[:, u, :], moved[:, u * P : (u + 1) * P], identity[:])
+            nc.scalar.copy(z_pairs[:, square, :], back[:].rearrange("p u j -> p j u"))
+        nc.vector.tensor_tensor(z_half[1][:].rearrange("p (c i) t -> p c t i", i=4),
+                                term1[:, :, halves[1]].rearrange("p t (c i) -> p c t i", i=4),
+                                term2[:, :, halves[1]].rearrange("p t (c i) -> p c t i", i=4), ALU.add)
 
         def second_product(index, t, cols):
             bank = new_bank(index)
-            product(bank[:, cols], t, z_codes[:, cols], z_scales[:, cols])
-            nc.scalar.activation(raw_win[t][:, cols], bank[:, cols], ACT.Copy, scale=0.0625 * 0.75)
-            nc.scalar.activation(gain_win[t][:, cols], bank[:, cols], ACT.Copy, scale=0.0625)
+            product(bank[:, cols], t, z_codes[:, cols], z_scale_rows[:, cols])
+            nc.scalar.activation(window_a[t][:, cols], bank[:, cols], ACT.Copy, scale=SIXTEENTH * OUT_FACTOR)
+            return bank
 
-        for u in (1, 0):
-            nc.vector.quantize_mx(z_codes[:, halves[u]].bitcast(FP8X4), z_scales[:, halves[u]], zb[u][:].rearrange("p j t -> p (j t)"))
-            second_product(u, 0, halves[u])
+        def fill_window_b(bank, t, cols):
+            nc.scalar.activation(window_b[t][:, cols], bank[:, cols], ACT.Copy, scale=SIXTEENTH)
+
+        z_pieces = [(halves[1], z_half[1][:])] + [(square, z_half[0][:, square, :]) for square in squares]
+        first_tile = []
+        for index, (cols, values) in zip(SECOND_FIRST_TILE_BANKS, z_pieces):
+            nc.vector.quantize_mx(z_codes[:, cols].bitcast(FP8X4), z_scale_rows[:, cols], values.rearrange("p j t -> p (j t)"))
+            first_tile.append((second_product(index, 0, cols), cols))
+        for bank, cols in first_tile:
+            fill_window_b(bank, 0, cols)
         for t in range(1, PACK):
-            second_product(t + 1, t, whole)
+            fill_window_b(second_product(t + 1, t, whole), t, whole)
 
         out_rows = out.rearrange("(p t) j -> p t j", t=PACK)
         for t in range(PACK):
-            scaled, win = raw_win[t], gain_win[t]
-            c = held.tile([P, S], F32, name=f"c{t}")
-            a = held.tile([P, S], F32, name=f"a2_{t}")
-            b = held.tile([P, S], F32, name=f"b2_{t}")
-            o = held.tile([P, S], F32, name=f"o{t}")
-            nc.vector.tensor_copy(c[:], scaled[:].indirect(n5_list[:]))
-            nc.vector.tensor_tensor(a[:], win[:].indirect(n4_list[:]), scaled[:, :S], ALU.mult)
-            if t < PACK - 1:
-                nc.vector.tensor_tensor(b[:], win[:].indirect(n6_list[:]), c[:], ALU.mult)
-                turned = new_bank(5 + t % 2)
-                for j in range(0, S, P):
-                    for k, term in enumerate((a, b)):
-                        nc.tensor.matmul(turned[:, j : j + P], term[:, j : j + P], identity[:], start=(k == 0), stop=(k == 1), is_transpose=True)
+            at_n5 = held.tile([P, S], F32, name=f"at_n5_{t}")
+            left = held.tile([P, S], F32, name=f"left{t}")
+            right = held.tile([P, S], F32, name=f"right{t}")
+            result = held.tile([P, S], F32, name=f"result{t}")
+            nc.vector.tensor_copy(at_n5[:], window_a[t][:].indirect(n5_list[:]))
+            nc.vector.tensor_tensor(left[:], window_b[t][:].indirect(n4_list[:]), window_a[t][:, :S], ALU.mult)
+            if t < LAST:
+                nc.vector.tensor_tensor(right[:], window_b[t][:].indirect(n6_list[:]), at_n5[:], ALU.mult)
                 summed = held.tile([P, S], F32, name=f"summed{t}")
-                nc.scalar.copy(summed[:], turned[:])
-                back = new_bank((7, 1)[t % 2])
-                for j in range(0, S, P):
-                    nc.tensor.transpose(back[:, j : j + P], summed[:, j : j + P], identity[:])
-                nc.scalar.copy(o[:], back[:])
-                nc.sync.dma_start(out_rows[:, t, :], o[:])
+                for index, cols in zip(TURN_BANKS, halves):
+                    turned = new_bank(index)
+                    for j in range(cols.start, cols.stop, P):
+                        for k, term in enumerate((left, right)):
+                            nc.tensor.matmul(turned[:, j : j + P], term[:, j : j + P], identity[:], start=(k == 0), stop=(k == 1), is_transpose=True)
+                    nc.scalar.copy(summed[:, cols], turned[:, cols])
+                for index, cols in zip(BACK_BANKS, halves):
+                    back = new_bank(index)
+                    for j in range(cols.start, cols.stop, P):
+                        nc.tensor.transpose(back[:, j : j + P], summed[:, j : j + P], identity[:])
+                    nc.scalar.copy(result[:, cols], back[:, cols])
+                nc.sync.dma_start(out_rows[:, t, :], result[:])
             else:
-                for u, cols in enumerate(halves):
-                    nc.vector.tensor_tensor(b[:, cols], win[:].indirect(n6_list[:, list_halves[u]]), c[:, cols], ALU.mult)
-                    nc.vector.tensor_tensor(o[:, cols], a[:, cols], b[:, cols], ALU.add)
-                    nc.sync.dma_start(out_rows[:, t, cols], o[:, cols])
+                for cols in halves:
+                    nc.vector.tensor_tensor(right[:, cols], window_b[t][:].indirect(n6_list[:, entries(cols)]), at_n5[:, cols], ALU.mult)
+                    nc.vector.tensor_tensor(result[:, cols], left[:, cols], right[:, cols], ALU.add)
+                    nc.sync.dma_start(out_rows[:, t, cols], result[:, cols])

from contextlib import ExitStack

import concourse.mybir as mybir
from concourse.masks import make_identity

F32 = mybir.dt.float32
BF16 = mybir.dt.bfloat16
I32 = mybir.dt.int32
U32 = mybir.dt.uint32
U16 = mybir.dt.uint16
U8 = mybir.dt.uint8
FP8X4 = mybir.dt.float8_e4m3fn_x4
ACT = mybir.ActivationFunctionType
ALU = mybir.AluOpType

P = 128
PACK = 4
LAST = PACK - 1
S = 512
HALF = S // 2
GROUP = 16
QUADRANT = 32
BLOCK_PARTITIONS = 8
TABLE = 2048
WINDOW = 2 * S
SIXTEENTH = 0.0625
OUT_FACTOR = 0.75

FIRST_TILE_BANKS = (0, 1)
TURN_BANKS = (5, 6)
BACK_BANKS = (7, 0)
SECOND_FIRST_TILE_BANKS = (1, 5, 6)

FLOPS = 2 * 2 * 512 * 512 * 512


def tile_picked_ringwsumdot_none_p_kernel(tc, x_words, x_scales, d_words, d_scales, gs, offs, k1, n1, n2, n3, n4, n5, n6, out):
    nc = tc.nc
    whole = slice(0, S)
    halves = [slice(0, HALF), slice(HALF, S)]
    squares = [slice(0, P), slice(P, 2 * P)]

    def entries(cols):
        return slice(cols.start // GROUP, cols.stop // GROUP)

    with ExitStack() as ctx:
        held = ctx.enter_context(tc.tile_pool(name="held", bufs=1))
        psum = ctx.enter_context(tc.psum_pool(name="psum", bufs=1))

        def load_list(name, src):
            tile = held.tile([P, S // GROUP], U16, name=name)
            nc.sync.dma_start(tile[:], src)
            return tile

        def load_words(name, src):
            tile = held.tile([P, TABLE], U32, name=name)
            nc.sync.dma_start(tile[:].bitcast(I32), src[0].rearrange("p n r -> p (n r)").bitcast(I32))
            return tile

        def new_bank(index, shape=(P, S)):
            return psum.tile(list(shape), F32, name=f"bank{index}")

        d_byte_table = held.tile([P, TABLE], U8, name="d_byte_table")
        x_byte_table = held.tile([P, TABLE], U8, name="x_byte_table")
        nc.gpsimd.memset(d_byte_table[:].bitcast(I32), 0)
        nc.vector.memset(x_byte_table[:].bitcast(I32), 0)
        nc.sync.dma_start(d_byte_table[0:P:BLOCK_PARTITIONS, :].bitcast(I32), d_scales[0].bitcast(I32))
        k1_list = load_list("k1_list", k1)
        offs_list = load_list("offs_list", offs)
        for q in range(P // QUADRANT):
            nc.sync.dma_start(x_byte_table[QUADRANT * q : QUADRANT * q + 4, :].bitcast(I32), x_scales[0, 4 * q : 4 * q + 4, :].bitcast(I32))
        d_word_table = load_words("d_word_table", d_words)
        x_word_table = load_words("x_word_table", x_words)
        n3_list = load_list("n3_list", n3)
        n1_list = load_list("n1_list", n1)
        n2_list = load_list("n2_list", n2)
        gs_cols = held.tile([P, PACK], F32, name="gs_cols")
        nc.gpsimd.dma_start(gs_cols[:], gs.rearrange("(p t) o -> p (t o)", t=PACK))
        gains = held.tile([P, PACK], F32, name="gains")
        nc.gpsimd.tensor_scalar(gains[:], gs_cols[:], SIXTEENTH, 0.0, ALU.mult, ALU.add)
        n5_list = load_list("n5_list", n5)
        n4_list = load_list("n4_list", n4)
        n6_list = load_list("n6_list", n6)

        d_scale_rows = held.tile([P, S], U8, name="d_scale_rows", align_bytes=64)

        window_a = [held.tile([P, WINDOW], F32, name=f"window_a{t}") for t in range(PACK)]
        window_b = [held.tile([P, WINDOW], F32, name=f"window_b{t}") for t in range(PACK)]
        for t in range(PACK):
            nc.gpsimd.memset(window_b[t][:, S:], 0.0)
        identity = held.tile([P, P], F32, name="identity")
        make_identity(nc, identity[:])

        d_bytes = held.tile([P, S], U8, name="d_bytes")
        x_scale_rows = held.tile([P, S], U8, name="x_scale_rows", align_bytes=64)
        nc.vector.tensor_copy(d_bytes[:], d_byte_table[:].indirect(k1_list[:]))
        nc.vector.tensor_copy(d_scale_rows[:].rearrange("p (t m) -> p m t", t=PACK), d_bytes[:].rearrange("p (m t) -> p m t", t=PACK))
        for r in range(1, 4):
            nc.scalar.dma_start(d_scale_rows[r:P:QUADRANT, :].bitcast(I32), d_scale_rows[BLOCK_PARTITIONS * r : P : QUADRANT, :].bitcast(I32))
        nc.vector.tensor_copy(x_scale_rows[:], x_byte_table[:].indirect(offs_list[:]))

        d_picked = held.tile([P, S], U32, name="d_picked")
        d_codes = held.tile([P, S], U32, name="d_codes", align_bytes=64)
        x_codes = held.tile([P, S], U32, name="x_codes", align_bytes=64)
        nc.vector.tensor_copy(d_picked[:], d_word_table[:].indirect(k1_list[:]))
        dealt = d_codes[:].rearrange("p (t m) -> p m t", t=PACK)
        picked = d_picked[:].rearrange("p (m t) -> p m t", t=PACK)
        nc.vector.tensor_copy(dealt[:, :, 0], picked[:, :, 0])
        for cols in halves:
            nc.vector.tensor_copy(x_codes[:, cols], x_word_table[:].indirect(offs_list[:, entries(cols)]))
        nc.vector.tensor_copy(dealt[:, :, 1:], picked[:, :, 1:])

        def product(bank, t, codes, scales):
            rows = slice(t * P, (t + 1) * P)
            nc.tensor.matmul_mx(bank, lhsT=d_codes[:, rows].bitcast(FP8X4), lhsT_scale=d_scale_rows[:, rows],
                                rhs=codes.bitcast(FP8X4), rhs_scale=scales, start=True, stop=True)

        term1 = held.tile([P, PACK, S], F32, name="term1")
        term2 = held.tile([P, PACK, S], F32, name="term2")

        def make_term1(t):
            sums = window_a[t][:, :S]
            sig = window_a[t][:, S:]
            weighted = window_b[t][:, :S]
            pieces = list(zip(FIRST_TILE_BANKS, halves)) if t == 0 else [(t + 1, whole)]
            for index, cols in pieces:
                bank = new_bank(index)
                product(bank[:, cols], t, x_codes[:, cols], x_scale_rows[:, cols])
                sigmoid_first = t == 0 and cols == halves[0]
                if sigmoid_first:
                    nc.scalar.activation(sig[:, cols], bank[:, cols], ACT.Sigmoid, scale=SIXTEENTH)
                nc.scalar.copy(sums[:, cols], bank[:, cols])
                if not sigmoid_first:
                    nc.scalar.activation(sig[:, cols], bank[:, cols], ACT.Sigmoid, scale=SIXTEENTH)
                if t < LAST:
                    nc.vector.tensor_scalar(weighted[:, cols], sums[:, cols], gains[:, t : t + 1], None, ALU.mult)
                else:
                    nc.scalar.activation(weighted[:, cols], bank[:, cols], ACT.Copy, scale=gains[:, t : t + 1])
            nc.vector.tensor_tensor(term1[:, t, :], window_b[t][:].indirect(n1_list[:]), sig, ALU.mult)

        turned_z = [new_bank(index, (P, PACK, P)) for index in TURN_BANKS]

        def make_term2(t):
            sig_n3 = held.tile([P, S], F32, name=f"sig_n3_{t}")
            nc.scalar.activation(sig_n3[:], window_a[t][:].indirect(n3_list[:]), ACT.Sigmoid, scale=SIXTEENTH)
            for cols in halves if t == LAST else [whole]:
                nc.vector.tensor_tensor(term2[:, t, cols], window_b[t][:].indirect(n2_list[:, entries(cols)]), sig_n3[:, cols], ALU.mult)
            for turned, square in zip(turned_z, squares):
                for k, term in enumerate((term1, term2)):
                    nc.tensor.matmul(turned[:, t, :], term[:, t, square], identity[:], start=(k == 0), stop=(k == 1), is_transpose=True)

        for t in range(PACK + 1):
            if t < PACK:
                make_term1(t)
            if t > 0:
                make_term2(t - 1)

        z_codes = held.tile([P, S], U32, name="z_codes", align_bytes=64)
        z_scale_rows = held.tile([P, S], U8, name="z_scale_rows", align_bytes=64)
        z_half = [held.tile([P, HALF, PACK], BF16, name=f"z_half{u}", align_bytes=64) for u in range(2)]
        pairs = [held.tile([P, 2, P, 2], BF16, name=f"pairs{i}") for i in range(2)]
        for paired, turned in zip(pairs, turned_z):
            nc.scalar.copy(paired[:], turned[:].rearrange("j (u e) p -> j u p e", e=2))
        z_pairs = z_half[0][:].rearrange("p j t -> p (j t)").bitcast(F32).rearrange("p (j u) -> p j u", u=2)
        for paired, index, square in zip(pairs, BACK_BANKS, squares):
            moved = paired[:].rearrange("j u p e -> j (u p e)").bitcast(F32)
            back = new_bank(index, (P, 2, P))
            for u in range(2):
                nc.tensor.transpose(back[:, u, :], moved[:, u * P : (u + 1) * P], identity[:])
            nc.scalar.copy(z_pairs[:, square, :], back[:].rearrange("p u j -> p j u"))
        nc.vector.tensor_tensor(z_half[1][:].rearrange("p (c i) t -> p c t i", i=4),
                                term1[:, :, halves[1]].rearrange("p t (c i) -> p c t i", i=4),
                                term2[:, :, halves[1]].rearrange("p t (c i) -> p c t i", i=4), ALU.add)

        def second_product(index, t, cols):
            bank = new_bank(index)
            product(bank[:, cols], t, z_codes[:, cols], z_scale_rows[:, cols])
            nc.scalar.activation(window_a[t][:, cols], bank[:, cols], ACT.Copy, scale=SIXTEENTH * OUT_FACTOR)
            return bank

        def fill_window_b(bank, t, cols):
            nc.scalar.activation(window_b[t][:, cols], bank[:, cols], ACT.Copy, scale=SIXTEENTH)

        z_pieces = [(halves[1], z_half[1][:])] + [(square, z_half[0][:, square, :]) for square in squares]
        first_tile = []
        for index, (cols, values) in zip(SECOND_FIRST_TILE_BANKS, z_pieces):
            nc.vector.quantize_mx(z_codes[:, cols].bitcast(FP8X4), z_scale_rows[:, cols], values.rearrange("p j t -> p (j t)"))
            first_tile.append((second_product(index, 0, cols), cols))
        for bank, cols in first_tile:
            fill_window_b(bank, 0, cols)
        for t in range(1, PACK):
            fill_window_b(second_product(t + 1, t, whole), t, whole)

        out_rows = out.rearrange("(p t) j -> p t j", t=PACK)
        for t in range(PACK):
            at_n5 = held.tile([P, S], F32, name=f"at_n5_{t}")
            left = held.tile([P, S], F32, name=f"left{t}")
            right = held.tile([P, S], F32, name=f"right{t}")
            result = held.tile([P, S], F32, name=f"result{t}")
            nc.vector.tensor_copy(at_n5[:], window_a[t][:].indirect(n5_list[:]))
            nc.vector.tensor_tensor(left[:], window_b[t][:].indirect(n4_list[:]), window_a[t][:, :S], ALU.mult)
            if t < LAST:
                nc.vector.tensor_tensor(right[:], window_b[t][:].indirect(n6_list[:]), at_n5[:], ALU.mult)
                summed = held.tile([P, S], F32, name=f"summed{t}")
                for index, cols in zip(TURN_BANKS, halves):
                    turned = new_bank(index)
                    for j in range(cols.start, cols.stop, P):
                        for k, term in enumerate((left, right)):
                            nc.tensor.matmul(turned[:, j : j + P], term[:, j : j + P], identity[:], start=(k == 0), stop=(k == 1), is_transpose=True)
                    nc.scalar.copy(summed[:, cols], turned[:, cols])
                for index, cols in zip(BACK_BANKS, halves):
                    back = new_bank(index)
                    for j in range(cols.start, cols.stop, P):
                        nc.tensor.transpose(back[:, j : j + P], summed[:, j : j + P], identity[:])
                    nc.scalar.copy(result[:, cols], back[:, cols])
                nc.sync.dma_start(out_rows[:, t, :], result[:])
            else:
                for cols in halves:
                    nc.vector.tensor_tensor(right[:, cols], window_b[t][:].indirect(n6_list[:, entries(cols)]), at_n5[:, cols], ALU.mult)
                    nc.vector.tensor_tensor(result[:, cols], left[:, cols], right[:, cols], ALU.add)
                    nc.sync.dma_start(out_rows[:, t, cols], result[:, cols])
